import numpy as np, ml_dtypes
CORES = [14,30,46,142,158,174,270,286,302,398,414,430]
N = 12
NB, B = 6, 64
def setup_inputs(rng):
    return {"x": rng.standard_normal((N, 128, NB * B), dtype=np.float32).astype(ml_dtypes.bfloat16), "wv": (rng.standard_normal((N, 128, 128), dtype=np.float32) / 16).astype(ml_dtypes.bfloat16), "wh": (rng.standard_normal((N, 128, 128), dtype=np.float32) / 16).astype(ml_dtypes.bfloat16)}
def setup_inputs_big(rng):
    d = setup_inputs(rng)
    for k in ("x",): d[k] = (d[k].astype(np.float32) * 1048576.0).astype(d[k].dtype)
    return d
def setup_inputs_small(rng):
    d = setup_inputs(rng)
    for k in ("x",): d[k] = (d[k].astype(np.float32) * (1 / 1048576.0)).astype(d[k].dtype)
    return d
def setup_inputs_apart(rng):
    d = setup_inputs(rng)
    f = (10.0 ** rng.permutation(np.linspace(-1.5, 1.5, N))).astype(np.float32).reshape(N, 1, 1)
    for k in ("x",): d[k] = (d[k].astype(np.float32) * f).astype(d[k].dtype)
    return d
def reference(x, wv, wh):
    X, WV, WH = x.astype(np.float64), wv.astype(np.float64), wh.astype(np.float64)
    h = np.zeros((N, NB, 128, B))
    for r in range(N):
        for c in range(NB):
            a = X[r][:, B * c:B * c + B].copy()
            if r: a += WV[r].T @ h[r - 1][c]
            if c: a += WH[r].T @ h[r][c - 1]
            h[r][c] = np.maximum(a, 0.0)
    return {"y": np.concatenate([h[:, c] for c in range(NB)], axis=2).astype(ml_dtypes.bfloat16)}

@@ -1,0 +1,244 @@
+from concourse.mybir import AluOpType
+
+P, NB, B = 128, 6, 64
+W = NB * B
+INW = 2 * P + W
+SIZES = (1, 2, 3, 3, 3)
+AWAY = True
+RET_SPLIT = 3
+NE = 8
+SMAX = max(SIZES)
+NPS = 8 if SMAX <= 4 else SMAX
+
+SCRATCH = {
+    "own": ("sbuf", [P, INW], "bfloat16"),
+    "back": ("sbuf", [P, W], "bfloat16"),
+    "inp": ("sbuf", [P, SMAX * INW], "bfloat16"),
+    "hh": ("sbuf", [P, SMAX * W], "bfloat16"),
+    "top": ("sbuf", [P, W], "bfloat16"),
+    "zf": ("sbuf", [P, B], "float32"),
+    "zb": ("sbuf", [P, B], "bfloat16"),
+    "tmp": ("sbuf", [P, B], "float32"),
+    "zi": ("sbuf", [P, P + 1], "bfloat16"),
+    "ed": ("dram", [P + 1, P], "bfloat16"),
+    "eye": ("sbuf", [P, P], "bfloat16"),
+}
+for _i in range(NPS):
+    SCRATCH["ps%d" % _i] = ("psum", [P, 512], "float32")
+
+SEMAPHORES = (["ld", "zs", "id1", "id2", "t2", "sent", "st", "ret0", "ret1"]
+              + ["in%d" % k for k in range(SMAX)] + ["top%d" % c for c in range(NB)]
+              + ["m%d" % k for k in range(SMAX)] + ["v%d" % k for k in range(SMAX)])
+
+
+def _groups():
+    out, r = [], 0
+    for s in SIZES:
+        out.append(tuple(range(r, r + s)))
+        r += s
+    return out
+
+
+def _links(topo, a, b):
+    if not topo.may_write(a, b):
+        return None
+    if topo.host(a) == topo.host(b) and topo.chip(a) == topo.chip(b):
+        return 0
+    if topo.rack(topo.host(a)) == topo.rack(topo.host(b)):
+        return 1 if (topo.mates(a, b) or topo.same_plane(a, b)) else 2
+    if topo.chip(a) == topo.chip(b):
+        return 1
+    t = a + (topo.chip(b) - topo.chip(a)) * topo.CORES_PER_CHIP
+    return 2 if (topo.mates(a, t) or topo.same_plane(a, t)) else 3
+
+
+def _workers(topo, cores, groups):
+    n = len(cores)
+    lk = [[_links(topo, cores[a], cores[b]) for b in range(n)] for a in range(n)]
+    best = [None]
+
+    def go(i, used, cost):
+        if best[0] is not None and cost >= best[0][0]:
+            return
+        if i == len(groups):
+            best[0] = (cost, used)
+            return
+        rows = groups[i]
+        for w in range(n - 1, -1, -1):
+            if w in used or ((w in rows) == (AWAY and rows != (0,))):
+                continue
+            step = 0 if i == 0 else lk[used[-1]][w]
+            ways = [lk[r][w] for r in rows if r != w] + [lk[w][r] for r in rows if r != w]
+            if step is None or None in ways:
+                continue
+            heavy = 10 if i == len(groups) - 1 else 1
+            go(i + 1, used + (w,), cost + 1000 * step + heavy * sum(ways))
+
+    go(0, (), 0)
+    return best[0][1]
+
+
+def _bits(mask, n):
+    out, got, b = 0, 0, 0
+    while got < n:
+        if (mask >> b) & 1:
+            out |= 1 << b
+            got += 1
+        b += 1
+    return out
+
+
+def rank_program(g, core, T, topo):
+    rank = T.rank_of(core)
+    if rank is None:
+        return
+    cores = T.cores
+    groups = _groups()
+    workers = _workers(topo, cores, groups)
+    home = [i for i, rows in enumerate(groups) if rank in rows][0]
+    job = workers.index(rank) if rank in workers else None
+    sem = T.sem
+    seen, sent, stored = {}, [0], [0]
+    queues = {"g": g, "t": g.tensor, "v": g.vector, "s": g.sync, "a": g.scalar}
+
+    def pieces(i):
+        return [(0, RET_SPLIT), (RET_SPLIT, NB)] if i == len(groups) - 1 else [(0, NB)]
+
+    def need(q, name, val):
+        if val > seen.get((q, name), 0):
+            seen[(q, name)] = val
+            queues[q].wait_ge(sem[name], val)
+
+    def send(dst, out_ap, in_ap, rsem):
+        rid, pid = topo.addr(dst, core)
+        g.remote_dma(out_ap, in_ap, remote_sem=sem[rsem], local_sem=sem.sent, pid=pid, routing_id=rid,
+                     dma_engine_mask=_bits(topo.mask(core, dst), NE))
+        sent[0] += NE
+
+    def store(j, a, b, src):
+        queues["sa"[j % 2]].dma_start(T.y[:, a * B:b * B], src).then_inc(sem.st, 16)
+        stored[0] += 16
+
+    at_home = job == home
+    rows = groups[job] if job is not None else ()
+    s = len(rows)
+    ko = rows.index(rank) if at_home else None
+    buf, o = (T.inp, ko * INW) if at_home else (T.own, 0)
+    nld = 48 if rank else 32
+    g.sync.dma_start(buf[:, o + 2 * P:o + INW], T.x[:, :]).then_inc(sem.ld, 16)
+    if rank:
+        g.scalar.dma_start(buf[:, o:o + P], T.wv[:, :]).then_inc(sem.ld, 16)
+    g.scalar.dma_start(buf[:, o + P:o + 2 * P], T.wh[:, :]).then_inc(sem.ld, 16)
+    if not at_home:
+        k = groups[home].index(rank)
+        lo = 0 if rank else P
+        need("g", "ld", nld)
+        send(cores[workers[home]], T.inp[:, k * INW + lo:(k + 1) * INW], T.own[:, lo:INW], "in%d" % k)
+
+    if job is not None:
+        last = job == len(groups) - 1
+        nb = 2 if 2 * s <= NPS else 1
+
+        def xb(k, c):
+            return T.inp[:, k * INW + 2 * P + c * B:k * INW + 2 * P + (c + 1) * B]
+
+        def hb(k, c):
+            return T.hh[:, k * W + c * B:k * W + (c + 1) * B]
+
+        def ps(k, c):
+            return T["ps%d" % (k * nb + c % nb)][:, 0:B]
+
+        chain = [(k, c) for c in range(NB) for k in range(s)]
+
+        if rows == (0,) and at_home:
+            g.vector.memset(T.zb[:, :], 0.0).then_inc(sem.zs, 1)
+            g.vector.memset(T.zf[:, :], 0.0).then_inc(sem.zs, 1)
+            need("v", "zs", 2)
+            need("v", "ld", nld)
+            need("t", "ld", nld)
+            g.vector.tensor_tensor(hb(0, 0), xb(0, 0), T.zb[:, :], AluOpType.max).then_inc(sem.v0, 1)
+            for c in range(1, NB):
+                need("t", "v0", c)
+                g.tensor.matmul(ps(0, c), T.inp[:, P:2 * P], hb(0, c - 1), True, True).then_inc(sem.m0, 1)
+                need("v", "m0", c)
+                g.vector.tensor_tensor(T.tmp[:, :], ps(0, c), xb(0, c), AluOpType.add).then_inc(sem.t2, 1)
+                need("v", "t2", c)
+                g.vector.tensor_tensor(hb(0, c), T.tmp[:, :], T.zf[:, :], AluOpType.max).then_inc(sem.v0, 1)
+        else:
+            g.vector.memset(T.zi[:, 0:1], 1.0).then_inc(sem.zs, 1)
+            g.vector.memset(T.zi[:, 1:P + 1], 0.0).then_inc(sem.zs, 1)
+            g.vector.memset(T.zf[:, :], 0.0).then_inc(sem.zs, 1)
+            need("s", "zs", 3)
+            g.sync.dma_start(T.ed[:, :], T.zi[:, :]).then_inc(sem.id1, 16)
+            need("s", "id1", 16)
+            g.sync.dma_start(T.eye[:, :], T.ed[0:P, :]).then_inc(sem.id2, 16)
+
+            done = {}
+
+            def ops(k, c):
+                return ["x"] + (["h"] if c else []) + (["v"] if rows[k] else [])
+
+            def issue(k, c, kind):
+                kinds = ops(k, c)
+                if k == ko:
+                    need("t", "ld", nld)
+                else:
+                    need("t", "in%d" % k, NE)
+                b0 = k * INW
+                if kind == "x":
+                    need("t", "id2", 16)
+                    need("t", "v%d" % k, c - nb + 1)
+                    lhsT, rhs = T.eye[:, :], xb(k, c)
+                elif kind == "h":
+                    need("t", "v%d" % k, c)
+                    lhsT, rhs = T.inp[:, b0 + P:b0 + 2 * P], hb(k, c - 1)
+                else:
+                    lhsT = T.inp[:, b0:b0 + P]
+                    if k:
+                        need("t", "v%d" % (k - 1), c + 1)
+                        rhs = hb(k - 1, c)
+                    else:
+                        need("t", "top%d" % c, NE)
+                        rhs = T.top[:, c * B:(c + 1) * B]
+                ins = g.tensor.matmul(ps(k, c), lhsT, rhs, kind == kinds[0], kind == kinds[-1])
+                if kind == kinds[-1]:
+                    ins.then_inc(sem["m%d" % k], 1)
+                done[(k, c, kind)] = True
+
+            def upto(k, c, n):
+                for kind in ops(k, c)[:n]:
+                    if (k, c, kind) not in done:
+                        issue(k, c, kind)
+
+            upto(0, 0, len(ops(0, 0)) - 1)
+            for i, (k, c) in enumerate(chain):
+                upto(k, c, 3)
+                if i + 1 < len(chain):
+                    k2, c2 = chain[i + 1]
+                    upto(k2, c2, len(ops(k2, c2)) - 1)
+
+            need("v", "zs", 3)
+            for k, c in chain:
+                need("v", "m%d" % k, c + 1)
+                g.vector.tensor_tensor(hb(k, c), ps(k, c), T.zf[:, :], AluOpType.max).then_inc(sem["v%d" % k], 1)
+
+        if not last:
+            nxt = cores[workers[job + 1]]
+            for c in range(NB):
+                need("g", "v%d" % (s - 1), c + 1)
+                send(nxt, T.top[:, c * B:(c + 1) * B], hb(s - 1, c), "top%d" % c)
+        for j, (a, b) in enumerate(pieces(job)):
+            for k in range(s):
+                if k != ko:
+                    need("g", "v%d" % k, b)
+                    send(cores[rows[k]], T.back[:, a * B:b * B], T.hh[:, k * W + a * B:k * W + b * B], "ret%d" % j)
+            if at_home:
+                need("sa"[j % 2], "v%d" % ko, b)
+                store(j, a, b, T.hh[:, ko * W + a * B:ko * W + b * B])
+
+    if not at_home:
+        for j, (a, b) in enumerate(pieces(home)):
+            need("sa"[j % 2], "ret%d" % j, NE)
+            store(j, a, b, T.back[:, a * B:b * B])
+    need("g", "sent", sent[0])
+    need("g", "st", stored[0])

@@ -3,9 +3,11 @@ from concourse.mybir import AluOpType
 P, NB, B = 128, 6, 64
 W = NB * B
 INW = 2 * P + W
+CUTS = (0, P + B, 2 * P + 2 * B, INW)
+CUT = CUTS[1]
 SIZES = (1, 2, 3, 3, 3)
 AWAY = True
-RET_SPLIT = 3
+RET_SPLIT = 2
 NE = 8
 SMAX = max(SIZES)
 NPS = 8 if SMAX <= 4 else SMAX
@@ -26,8 +28,9 @@ SCRATCH = {
 for _i in range(NPS):
     SCRATCH["ps%d" % _i] = ("psum", [P, 512], "float32")
 
-SEMAPHORES = (["ld", "zs", "id1", "id2", "t2", "sent", "st", "ret0", "ret1"]
-              + ["in%d" % k for k in range(SMAX)] + ["top%d" % c for c in range(NB)]
+SEMAPHORES = (["lda", "ldb", "zs", "id1", "id2", "t2", "sent", "st", "ret0", "ret1"]
+              + ["in%d_%d" % (k, i) for k in range(SMAX) for i in range(3)]
+              + ["top%d" % c for c in range(NB)]
               + ["m%d" % k for k in range(SMAX)] + ["v%d" % k for k in range(SMAX)])
 
 
@@ -56,23 +59,24 @@ def _workers(topo, cores, groups):
     n = len(cores)
     lk = [[_links(topo, cores[a], cores[b]) for b in range(n)] for a in range(n)]
     best = [None]
+    end = len(groups) - 1
 
     def go(i, used, cost):
         if best[0] is not None and cost >= best[0][0]:
             return
-        if i == len(groups):
+        if i > end:
             best[0] = (cost, used)
             return
         rows = groups[i]
         for w in range(n - 1, -1, -1):
-            if w in used or ((w in rows) == (AWAY and rows != (0,))):
+            if w in used or ((w in rows) == (AWAY and 0 < i < end)) or (i < end and w == n - 1):
                 continue
             step = 0 if i == 0 else lk[used[-1]][w]
             ways = [lk[r][w] for r in rows if r != w] + [lk[w][r] for r in rows if r != w]
             if step is None or None in ways:
                 continue
-            heavy = 10 if i == len(groups) - 1 else 1
-            go(i + 1, used + (w,), cost + 1000 * step + heavy * sum(ways))
+            heavy = 10 if i == end else 1
+            go(i + 1, used + (w,), cost + 1000 * step + heavy * sum(ways) + (n - 1 - w if i == end else 0))
 
     go(0, (), 0)
     return best[0][1]
@@ -124,23 +128,30 @@ def rank_program(g, core, T, topo):
     s = len(rows)
     ko = rows.index(rank) if at_home else None
     buf, o = (T.inp, ko * INW) if at_home else (T.own, 0)
-    nld = 48 if rank else 32
-    g.sync.dma_start(buf[:, o + 2 * P:o + INW], T.x[:, :]).then_inc(sem.ld, 16)
+    nla = 32 if rank else 16
+    g.sync.dma_start(buf[:, o + P:o + CUT], T.x[:, 0:B]).then_inc(sem.lda, 16)
     if rank:
-        g.scalar.dma_start(buf[:, o:o + P], T.wv[:, :]).then_inc(sem.ld, 16)
-    g.scalar.dma_start(buf[:, o + P:o + 2 * P], T.wh[:, :]).then_inc(sem.ld, 16)
+        g.scalar.dma_start(buf[:, o:o + P], T.wv[:, :]).then_inc(sem.lda, 16)
+    g.sync.dma_start(buf[:, o + CUT + P:o + INW], T.x[:, B:W]).then_inc(sem.ldb, 16)
+    g.scalar.dma_start(buf[:, o + CUT:o + CUT + P], T.wh[:, :]).then_inc(sem.ldb, 16)
     if not at_home:
         k = groups[home].index(rank)
-        lo = 0 if rank else P
-        need("g", "ld", nld)
-        send(cores[workers[home]], T.inp[:, k * INW + lo:(k + 1) * INW], T.own[:, lo:INW], "in%d" % k)
+        for i in range(3):
+            lo = CUTS[i] if (rank or i) else P
+            if i == 0:
+                need("g", "lda", nla)
+            else:
+                need("g", "ldb", 32)
+            send(cores[workers[home]], T.inp[:, k * INW + lo:k * INW + CUTS[i + 1]], T.own[:, lo:CUTS[i + 1]],
+                 "in%d_%d" % (k, i))
 
     if job is not None:
         last = job == len(groups) - 1
         nb = 2 if 2 * s <= NPS else 1
 
         def xb(k, c):
-            return T.inp[:, k * INW + 2 * P + c * B:k * INW + 2 * P + (c + 1) * B]
+            a = k * INW + (CUT + P + (c - 1) * B if c else P)
+            return T.inp[:, a:a + B]
 
         def hb(k, c):
             return T.hh[:, k * W + c * B:k * W + (c + 1) * B]
@@ -148,18 +159,25 @@ def rank_program(g, core, T, topo):
         def ps(k, c):
             return T["ps%d" % (k * nb + c % nb)][:, 0:B]
 
+        def have(q, k, i):
+            if k == ko:
+                need(q, "ldb" if i else "lda", 32 if i else nla)
+            else:
+                need(q, "in%d_%d" % (k, i), NE)
+
         chain = [(k, c) for c in range(NB) for k in range(s)]
 
         if rows == (0,) and at_home:
             g.vector.memset(T.zb[:, :], 0.0).then_inc(sem.zs, 1)
             g.vector.memset(T.zf[:, :], 0.0).then_inc(sem.zs, 1)
             need("v", "zs", 2)
-            need("v", "ld", nld)
-            need("t", "ld", nld)
+            have("v", 0, 0)
             g.vector.tensor_tensor(hb(0, 0), xb(0, 0), T.zb[:, :], AluOpType.max).then_inc(sem.v0, 1)
+            have("v", 0, 1)
+            have("t", 0, 1)
             for c in range(1, NB):
                 need("t", "v0", c)
-                g.tensor.matmul(ps(0, c), T.inp[:, P:2 * P], hb(0, c - 1), True, True).then_inc(sem.m0, 1)
+                g.tensor.matmul(ps(0, c), T.inp[:, CUT:CUT + P], hb(0, c - 1), True, True).then_inc(sem.m0, 1)
                 need("v", "m0", c)
                 g.vector.tensor_tensor(T.tmp[:, :], ps(0, c), xb(0, c), AluOpType.add).then_inc(sem.t2, 1)
                 need("v", "t2", c)
@@ -180,19 +198,18 @@ def rank_program(g, core, T, topo):
 
             def issue(k, c, kind):
                 kinds = ops(k, c)
-                if k == ko:
-                    need("t", "ld", nld)
-                else:
-                    need("t", "in%d" % k, NE)
                 b0 = k * INW
                 if kind == "x":
+                    have("t", k, min(c, 2))
                     need("t", "id2", 16)
                     need("t", "v%d" % k, c - nb + 1)
                     lhsT, rhs = T.eye[:, :], xb(k, c)
                 elif kind == "h":
+                    have("t", k, 1)
                     need("t", "v%d" % k, c)
-                    lhsT, rhs = T.inp[:, b0 + P:b0 + 2 * P], hb(k, c - 1)
+                    lhsT, rhs = T.inp[:, b0 + CUT:b0 + CUT + P], hb(k, c - 1)
                 else:
+                    have("t", k, 0)
                     lhsT = T.inp[:, b0:b0 + P]
                     if k:
                         need("t", "v%d" % (k - 1), c + 1)

@@ -165,7 +165,7 @@ def rank_program(g, core, T, topo):
             else:
                 need(q, "in%d_%d" % (k, i), NE)
 
-        chain = [(k, c) for c in range(NB) for k in range(s)]
+        chain = sorted([(k, c) for c in range(NB) for k in range(s)], key=lambda b: (b[0] + b[1], -b[0]))
 
         if rows == (0,) and at_home:
             g.vector.memset(T.zb[:, :], 0.0).then_inc(sem.zs, 1)

from concourse.mybir import AluOpType

P, NB, B = 128, 6, 64
W = NB * B
INW = 2 * P + W
CUTS = (0, P + B, 2 * P + 2 * B, INW)
CUT = CUTS[1]
SIZES = (1, 2, 3, 3, 3)
AWAY = True
RET_SPLIT = 2
NE = 8
SMAX = max(SIZES)
NPS = 8 if SMAX <= 4 else SMAX

SCRATCH = {
    "own": ("sbuf", [P, INW], "bfloat16"),
    "back": ("sbuf", [P, W], "bfloat16"),
    "inp": ("sbuf", [P, SMAX * INW], "bfloat16"),
    "hh": ("sbuf", [P, SMAX * W], "bfloat16"),
    "top": ("sbuf", [P, W], "bfloat16"),
    "zf": ("sbuf", [P, B], "float32"),
    "zb": ("sbuf", [P, B], "bfloat16"),
    "tmp": ("sbuf", [P, B], "float32"),
    "zi": ("sbuf", [P, P + 1], "bfloat16"),
    "ed": ("dram", [P + 1, P], "bfloat16"),
    "eye": ("sbuf", [P, P], "bfloat16"),
}
for _i in range(NPS):
    SCRATCH["ps%d" % _i] = ("psum", [P, 512], "float32")

SEMAPHORES = (["lda", "ldb", "zs", "id1", "id2", "t2", "sent", "st", "ret0", "ret1"]
              + ["in%d_%d" % (k, i) for k in range(SMAX) for i in range(3)]
              + ["top%d" % c for c in range(NB)]
              + ["m%d" % k for k in range(SMAX)] + ["v%d" % k for k in range(SMAX)])


def _groups():
    out, r = [], 0
    for s in SIZES:
        out.append(tuple(range(r, r + s)))
        r += s
    return out


def _links(topo, a, b):
    if not topo.may_write(a, b):
        return None
    if topo.host(a) == topo.host(b) and topo.chip(a) == topo.chip(b):
        return 0
    if topo.rack(topo.host(a)) == topo.rack(topo.host(b)):
        return 1 if (topo.mates(a, b) or topo.same_plane(a, b)) else 2
    if topo.chip(a) == topo.chip(b):
        return 1
    t = a + (topo.chip(b) - topo.chip(a)) * topo.CORES_PER_CHIP
    return 2 if (topo.mates(a, t) or topo.same_plane(a, t)) else 3


def _workers(topo, cores, groups):
    n = len(cores)
    lk = [[_links(topo, cores[a], cores[b]) for b in range(n)] for a in range(n)]
    best = [None]
    end = len(groups) - 1

    def go(i, used, cost):
        if best[0] is not None and cost >= best[0][0]:
            return
        if i > end:
            best[0] = (cost, used)
            return
        rows = groups[i]
        for w in range(n - 1, -1, -1):
            if w in used or ((w in rows) == (AWAY and 0 < i < end)) or (i < end and w == n - 1):
                continue
            step = 0 if i == 0 else lk[used[-1]][w]
            ways = [lk[r][w] for r in rows if r != w] + [lk[w][r] for r in rows if r != w]
            if step is None or None in ways:
                continue
            heavy = 10 if i == end else 1
            go(i + 1, used + (w,), cost + 1000 * step + heavy * sum(ways) + (n - 1 - w if i == end else 0))

    go(0, (), 0)
    return best[0][1]


def _bits(mask, n):
    out, got, b = 0, 0, 0
    while got < n:
        if (mask >> b) & 1:
            out |= 1 << b
            got += 1
        b += 1
    return out


def rank_program(g, core, T, topo):
    rank = T.rank_of(core)
    if rank is None:
        return
    cores = T.cores
    groups = _groups()
    workers = _workers(topo, cores, groups)
    home = [i for i, rows in enumerate(groups) if rank in rows][0]
    job = workers.index(rank) if rank in workers else None
    sem = T.sem
    seen, sent, stored = {}, [0], [0]
    queues = {"g": g, "t": g.tensor, "v": g.vector, "s": g.sync, "a": g.scalar}

    def pieces(i):
        return [(0, RET_SPLIT), (RET_SPLIT, NB)] if i == len(groups) - 1 else [(0, NB)]

    def need(q, name, val):
        if val > seen.get((q, name), 0):
            seen[(q, name)] = val
            queues[q].wait_ge(sem[name], val)

    def send(dst, out_ap, in_ap, rsem):
        rid, pid = topo.addr(dst, core)
        g.remote_dma(out_ap, in_ap, remote_sem=sem[rsem], local_sem=sem.sent, pid=pid, routing_id=rid,
                     dma_engine_mask=_bits(topo.mask(core, dst), NE))
        sent[0] += NE

    def store(j, a, b, src):
        queues["sa"[j % 2]].dma_start(T.y[:, a * B:b * B], src).then_inc(sem.st, 16)
        stored[0] += 16

    at_home = job == home
    rows = groups[job] if job is not None else ()
    s = len(rows)
    ko = rows.index(rank) if at_home else None
    buf, o = (T.inp, ko * INW) if at_home else (T.own, 0)
    nla = 32 if rank else 16
    g.sync.dma_start(buf[:, o + P:o + CUT], T.x[:, 0:B]).then_inc(sem.lda, 16)
    if rank:
        g.scalar.dma_start(buf[:, o:o + P], T.wv[:, :]).then_inc(sem.lda, 16)
    g.sync.dma_start(buf[:, o + CUT + P:o + INW], T.x[:, B:W]).then_inc(sem.ldb, 16)
    g.scalar.dma_start(buf[:, o + CUT:o + CUT + P], T.wh[:, :]).then_inc(sem.ldb, 16)
    if not at_home:
        k = groups[home].index(rank)
        for i in range(3):
            lo = CUTS[i] if (rank or i) else P
            if i == 0:
                need("g", "lda", nla)
            else:
                need("g", "ldb", 32)
            send(cores[workers[home]], T.inp[:, k * INW + lo:k * INW + CUTS[i + 1]], T.own[:, lo:CUTS[i + 1]],
                 "in%d_%d" % (k, i))

    if job is not None:
        last = job == len(groups) - 1
        nb = 2 if 2 * s <= NPS else 1

        def xb(k, c):
            a = k * INW + (CUT + P + (c - 1) * B if c else P)
            return T.inp[:, a:a + B]

        def hb(k, c):
            return T.hh[:, k * W + c * B:k * W + (c + 1) * B]

        def ps(k, c):
            return T["ps%d" % (k * nb + c % nb)][:, 0:B]

        def have(q, k, i):
            if k == ko:
                need(q, "ldb" if i else "lda", 32 if i else nla)
            else:
                need(q, "in%d_%d" % (k, i), NE)

        chain = sorted([(k, c) for c in range(NB) for k in range(s)], key=lambda b: (b[0] + b[1], -b[0]))

        if rows == (0,) and at_home:
            g.vector.memset(T.zb[:, :], 0.0).then_inc(sem.zs, 1)
            g.vector.memset(T.zf[:, :], 0.0).then_inc(sem.zs, 1)
            need("v", "zs", 2)
            have("v", 0, 0)
            g.vector.tensor_tensor(hb(0, 0), xb(0, 0), T.zb[:, :], AluOpType.max).then_inc(sem.v0, 1)
            have("v", 0, 1)
            have("t", 0, 1)
            for c in range(1, NB):
                need("t", "v0", c)
                g.tensor.matmul(ps(0, c), T.inp[:, CUT:CUT + P], hb(0, c - 1), True, True).then_inc(sem.m0, 1)
                need("v", "m0", c)
                g.vector.tensor_tensor(T.tmp[:, :], ps(0, c), xb(0, c), AluOpType.add).then_inc(sem.t2, 1)
                need("v", "t2", c)
                g.vector.tensor_tensor(hb(0, c), T.tmp[:, :], T.zf[:, :], AluOpType.max).then_inc(sem.v0, 1)
        else:
            g.vector.memset(T.zi[:, 0:1], 1.0).then_inc(sem.zs, 1)
            g.vector.memset(T.zi[:, 1:P + 1], 0.0).then_inc(sem.zs, 1)
            g.vector.memset(T.zf[:, :], 0.0).then_inc(sem.zs, 1)
            need("s", "zs", 3)
            g.sync.dma_start(T.ed[:, :], T.zi[:, :]).then_inc(sem.id1, 16)
            need("s", "id1", 16)
            g.sync.dma_start(T.eye[:, :], T.ed[0:P, :]).then_inc(sem.id2, 16)

            done = {}

            def ops(k, c):
                return ["x"] + (["h"] if c else []) + (["v"] if rows[k] else [])

            def issue(k, c, kind):
                kinds = ops(k, c)
                b0 = k * INW
                if kind == "x":
                    have("t", k, min(c, 2))
                    need("t", "id2", 16)
                    need("t", "v%d" % k, c - nb + 1)
                    lhsT, rhs = T.eye[:, :], xb(k, c)
                elif kind == "h":
                    have("t", k, 1)
                    need("t", "v%d" % k, c)
                    lhsT, rhs = T.inp[:, b0 + CUT:b0 + CUT + P], hb(k, c - 1)
                else:
                    have("t", k, 0)
                    lhsT = T.inp[:, b0:b0 + P]
                    if k:
                        need("t", "v%d" % (k - 1), c + 1)
                        rhs = hb(k - 1, c)
                    else:
                        need("t", "top%d" % c, NE)
                        rhs = T.top[:, c * B:(c + 1) * B]
                ins = g.tensor.matmul(ps(k, c), lhsT, rhs, kind == kinds[0], kind == kinds[-1])
                if kind == kinds[-1]:
                    ins.then_inc(sem["m%d" % k], 1)
                done[(k, c, kind)] = True

            def upto(k, c, n):
                for kind in ops(k, c)[:n]:
                    if (k, c, kind) not in done:
                        issue(k, c, kind)

            upto(0, 0, len(ops(0, 0)) - 1)
            for i, (k, c) in enumerate(chain):
                upto(k, c, 3)
                if i + 1 < len(chain):
                    k2, c2 = chain[i + 1]
                    upto(k2, c2, len(ops(k2, c2)) - 1)

            need("v", "zs", 3)
            for k, c in chain:
                need("v", "m%d" % k, c + 1)
                g.vector.tensor_tensor(hb(k, c), ps(k, c), T.zf[:, :], AluOpType.max).then_inc(sem["v%d" % k], 1)

        if not last:
            nxt = cores[workers[job + 1]]
            for c in range(NB):
                need("g", "v%d" % (s - 1), c + 1)
                send(nxt, T.top[:, c * B:(c + 1) * B], hb(s - 1, c), "top%d" % c)
        for j, (a, b) in enumerate(pieces(job)):
            for k in range(s):
                if k != ko:
                    need("g", "v%d" % k, b)
                    send(cores[rows[k]], T.back[:, a * B:b * B], T.hh[:, k * W + a * B:k * W + b * B], "ret%d" % j)
            if at_home:
                need("sa"[j % 2], "v%d" % ko, b)
                store(j, a, b, T.hh[:, ko * W + a * B:ko * W + b * B])

    if not at_home:
        for j, (a, b) in enumerate(pieces(home)):
            need("sa"[j % 2], "ret%d" % j, NE)
            store(j, a, b, T.back[:, a * B:b * B])
    need("g", "sent", sent[0])
    need("g", "st", stored[0])
